import numpy as np
import ml_dtypes


def mxq(x, axis, fmt="e4m3"):
    dtype, down = {"e4m3": (ml_dtypes.float8_e4m3fn, 7), "e5m2": (ml_dtypes.float8_e5m2, 14)}[fmt]
    v = np.moveaxis(np.asarray(x, np.float32).astype(ml_dtypes.bfloat16).astype(np.float64), axis, -1)
    blocks = v.reshape(v.shape[:-1] + (-1, 32))
    amax = np.abs(blocks).max(-1, keepdims=True)
    byte = np.maximum(np.where(amax > 0, np.frexp(amax)[1] - 1 + 127, 0) - down, 1)
    scale = np.exp2(byte - 127.0)
    codes = (blocks / scale).astype(np.float32).astype(dtype).astype(np.float64)
    return np.moveaxis((codes * scale).reshape(v.shape), -1, axis)


WIDE = False


def mx_kscale(k):
    if not WIDE:
        return np.ones(k)
    levels = np.array([10, -10, 5, -5, 0])
    if k % 512:
        return np.exp2(np.random.permutation(np.resize(levels, k // 32))).repeat(32)
    a = np.empty((k // 512, 16))
    for p in range(k // 512):
        a[p, :8] = np.random.permutation(np.resize(levels, 8))
        for g in range(8):
            far = levels[np.abs(levels - a[p, g]) >= 10]
            a[p, g + 8] = far[np.random.randint(len(far))]
    return np.exp2(a.ravel()).repeat(32)


def f64(x):
    return np.asarray(x).astype(np.float64)


def striped(idx):
    return np.tile(idx.reshape(-1, 16).T, (8, 1)).astype(np.uint16)


def unstriped(offs):
    return offs[:16].T.reshape(-1).astype(np.int64)


E2M1 = np.array([0.0, 0.5, 1.0, 1.5, 2.0, 3.0, 4.0, 6.0, -0.0, -0.5, -1.0, -1.5, -2.0, -3.0, -4.0, -6.0])


def pack_weight(w, fmt):
    k, n = w.shape
    w = f64(np.asarray(w, np.float32).astype(ml_dtypes.bfloat16)).reshape(k // 32, 32, n)
    amax = np.abs(w).max(1)
    if fmt == "e4m3":
        byte = np.frexp(amax)[1] - 1 + 127 - 7
    else:
        mant, ex = np.frexp(amax / 6.0)
        byte = np.where(mant > 0.5, ex, ex - 1) + 127
    byte = np.clip(np.where(amax > 0, byte, 1), 1, 254)
    scaled = (w * np.exp2(127.0 - byte)[:, None, :]).reshape(k, n).astype(np.float32)
    by_word = np.ascontiguousarray(scaled.reshape(k // 512, 128, 4, n).transpose(0, 1, 3, 2))
    if fmt == "e4m3":
        words = by_word.astype(ml_dtypes.float8_e4m3fn).view(np.uint8)
    else:
        c = by_word.astype(ml_dtypes.float4_e2m1fn).view(np.uint8) & 0xF
        words = (c[..., 0::2] | (c[..., 1::2] << 4)).reshape(k // 512, 128, 2 * n)
    return np.ascontiguousarray(words), np.ascontiguousarray(byte.astype(np.uint8).reshape(k // 512, 16, n))


def unpack_weight(words, scales, fmt):
    g, _, n = scales.shape
    words = np.ascontiguousarray(words).reshape(g, 128, n, -1)
    if fmt == "e4m3":
        vals = words.view(ml_dtypes.float8_e4m3fn).astype(np.float64)
    else:
        nib = np.empty((g, 128, n, 4), np.uint8)
        nib[..., 0::2] = words & 0xF
        nib[..., 1::2] = words >> 4
        vals = E2M1[nib]
    vals = vals * np.repeat(np.exp2(scales.astype(np.float64) - 127.0), 8, axis=1)[..., None]
    return vals.transpose(0, 1, 3, 2).reshape(g * 512, n)


def pack_table(v):
    words, scales = pack_weight(v, "e4m3")
    return np.concatenate([words.reshape(words.shape[0], -1), scales.reshape(scales.shape[0], -1)], axis=1)


def unpack_table(tab):
    g, t = tab.shape[0], tab.shape[1] // 528
    return unpack_weight(tab[:, :512 * t].reshape(g, 128, t, 4), tab[:, 512 * t:].reshape(g, 16, t), "e4m3")


def gelu(v):
    return 0.5 * v * (1.0 + np.tanh(np.sqrt(2.0 / np.pi) * (v + 0.044715 * v**3)))


K, M, T, S = 1536, 512, 4096, 2048


def setup_inputs():
    n = np.random.standard_normal
    s = mx_kscale(K)[:, None]
    return {
        "tab": pack_table(n((K, T)) * s),
        "w": (n((K, M)) / np.sqrt(K) / s).astype(np.float32),
        "b": (0.3 * n(512)).astype(np.float32),
        "offs": striped(np.random.permutation(T)[:S]),
    }


def reference(tab, w, b, offs):
    tab_ = unpack_table(tab)[:, unstriped(offs)]
    w_ = mxq(f64(w), 0, "e4m3")
    y = tab_.T @ w_
    return gelu(y + f64(b)[None, :])

@@ -1,0 +1,149 @@
+from contextlib import ExitStack
+
+import concourse.mybir as mybir
+from concourse.masks import make_identity
+
+F32 = mybir.dt.float32
+BF16 = mybir.dt.bfloat16
+I32 = mybir.dt.int32
+U32 = mybir.dt.uint32
+U16 = mybir.dt.uint16
+U8 = mybir.dt.uint8
+FP8X4 = mybir.dt.float8_e4m3fn_x4
+ADD = mybir.AluOpType.add
+MULT = mybir.AluOpType.mult
+GELU = mybir.ActivationFunctionType.Gelu_apprx_tanh
+
+K, N, T, S = 1536, 512, 4096, 2048
+P = 128
+PASSES = K // 512
+TILES = S // P
+BANKS = 8
+FLOPS = 2 * K * N * S
+
+
+def tile_list_tabw_tm_gelu_kernel(tc, tab, w, b, offs, out):
+    nc = tc.nc
+    with ExitStack() as ctx:
+        keep = ctx.enter_context(tc.tile_pool(name="keep", bufs=1))
+        stage = ctx.enter_context(tc.tile_pool(name="stage", bufs=8))
+        psum = ctx.enter_context(tc.psum_pool(name="psum", bufs=BANKS))
+
+        offsets = keep.tile([P, S // 16], U16, name="offsets")
+        planes = keep.tile([P, T], U8, align_bytes=64, name="planes")
+        words = [keep.tile([P, T], I32, align_bytes=64, name=f"words{a}") for a in range(PASSES)]
+        w_raw = [keep.tile([P, 4, N], F32, align_bytes=64, name=f"w_raw{a}") for a in range(PASSES)]
+        w_grp = [keep.tile([P, N, 4], BF16, align_bytes=64, name=f"w_grp{a}") for a in range(PASSES)]
+        w_codes = [keep.tile([P, N], U32, align_bytes=64, name=f"w_codes{a}") for a in range(PASSES)]
+        w_scales = [keep.tile([P, N], U8, align_bytes=64, name=f"w_scales{a}") for a in range(PASSES)]
+        g_words = [keep.tile([P, S], U32, align_bytes=64, name=f"g_words{a}") for a in range(PASSES)]
+        g_planes = keep.tile([P, S], U8, align_bytes=64, name="g_planes")
+        bias = keep.tile([P, N], F32, align_bytes=64, name="bias")
+        b_rows = keep.tile([P, P], F32, align_bytes=64, name="b_rows")
+        b_cols = keep.tile([P, N // P], F32, align_bytes=64, name="b_cols")
+        ident = keep.tile([P, P], F32, align_bytes=64, name="ident")
+        warm = keep.tile([P, 1], F32, name="warm")
+
+        nc.vector.memset(planes[:, 0:2560].bitcast(I32), 0)
+        nc.gpsimd.memset(planes[:, 2560:T].bitcast(I32), 0)
+        nc.gpsimd.memset(b_rows[:], 0.0)
+        nc.gpsimd.memset(warm[:], 0.0)
+        make_identity(nc, ident[:])
+        nc.sync.dma_start(offsets[:], offs)
+        scale_rows = tab[:, 512 * T : 528 * T].rearrange("a (q t) -> a q t", t=T)
+        for quad in range(4):
+            queue = nc.sync if quad < 2 else nc.scalar
+            queue.dma_start(
+                out=planes[32 * quad : 32 * quad + 4 * PASSES, :].bitcast(I32),
+                in_=scale_rows[:, 4 * quad : 4 * quad + 4, :].bitcast(I32),
+            )
+
+        def load_words(a):
+            nc.sync.dma_start(out=words[a][:], in_=tab[a, 0 : 512 * T].rearrange("(p x) -> p x", p=P).bitcast(I32))
+
+        def load_w(a):
+            nc.sync.dma_start(out=w_raw[a][:], in_=w[512 * a : 512 * (a + 1), :].rearrange("(p j) n -> p j n", j=4))
+
+        nc.scalar.activation(warm[:], warm[:], GELU)
+        load_words(0)
+        nc.scalar.dma_start(out=b_rows[0 : N // P, :], in_=b.rearrange("(c p) -> c p", p=P))
+        load_words(1)
+        load_w(0)
+        load_words(2)
+        load_w(1)
+        load_w(2)
+
+        turned = psum.tile([P, N], F32, name="acc")
+        nc.tensor.transpose(turned[:, 0:P], b_rows[:], ident[:])
+        nc.scalar.copy(b_cols[:], turned[:, 0 : N // P])
+        spread = psum.tile([P, N], F32, name="acc")
+        for c in range(N // P):
+            nc.tensor.transpose(spread[:, P * c : P * (c + 1)], b_cols[:, c : c + 1].to_broadcast([P, P]), ident[:])
+        nc.scalar.copy(bias[:], spread[:])
+
+        def gather_planes(j0, j1):
+            nc.vector.tensor_copy(g_planes[:, j0:j1], planes[:].indirect(offsets[:, j0 // 16 : j1 // 16]))
+
+        def gather_words(a, j0, j1):
+            nc.vector.tensor_copy(g_words[a][:, j0:j1], words[a][:].bitcast(U32).indirect(offsets[:, j0 // 16 : j1 // 16]))
+
+        def group(engine_copy, a, n0, n1):
+            engine_copy(
+                w_grp[a][:, n0:n1, :].rearrange("p (c i) t -> p c t i", i=4),
+                w_raw[a][:, :, n0:n1].rearrange("p t (c i) -> p c t i", i=4),
+            )
+
+        def pool_copy(dst, src):
+            nc.gpsimd.tensor_scalar(dst, src, 1.0, 0.0, MULT, ADD)
+
+        def quantize(a):
+            nc.vector.quantize_mx(
+                out=w_codes[a][:].bitcast(FP8X4), scales=w_scales[a][:], in_=w_grp[a][:].rearrange("p n t -> p (n t)")
+            )
+
+        def multiply(acc, i, a):
+            cols = slice(P * i, P * (i + 1))
+            nc.tensor.matmul_mx(
+                out=acc[:],
+                lhsT=g_words[a][:, cols].bitcast(FP8X4),
+                lhsT_scale=g_planes[4 * a : P, cols],
+                rhs=w_codes[a][:].bitcast(FP8X4),
+                rhs_scale=w_scales[a][:],
+                start=(a == 0),
+                stop=(a == PASSES - 1),
+            )
+
+        gather_planes(0, S)
+        gather_words(0, 0, S)
+        gather_words(1, 0, S)
+        group(nc.scalar.copy, 0, 0, N)
+        quantize(0)
+        accs = [psum.tile([P, N], F32, name="acc") for i in range(BANKS)]
+        for i in range(BANKS):
+            multiply(accs[i], i, 0)
+        for j0 in range(0, S, 512):
+            gather_words(2, j0, j0 + 512)
+        group(nc.scalar.copy, 1, 0, 400)
+        group(pool_copy, 1, 400, N)
+        quantize(1)
+        for i in range(BANKS):
+            multiply(accs[i], i, 1)
+        group(nc.scalar.copy, 2, 0, 400)
+        group(pool_copy, 2, 400, N)
+        quantize(2)
+        for i in range(TILES):
+            if i < BANKS:
+                acc = accs[i]
+            else:
+                acc = psum.tile([P, N], F32, name="acc")
+                multiply(acc, i, 0)
+                multiply(acc, i, 1)
+            multiply(acc, i, 2)
+            parts = 1 if i < TILES - 1 else 2
+            for c in range(parts):
+                cols = slice(N // parts * c, N // parts * (c + 1))
+                summed = stage.tile([P, N // parts], F32, name="summed")
+                nc.vector.tensor_tensor(summed[:], acc[:, cols], bias[:, cols], ADD)
+                result = stage.tile([P, N // parts], F32, name="result")
+                nc.scalar.activation(result[:], summed[:], GELU)
+                nc.sync.dma_start(out=out[P * i : P * (i + 1), cols], in_=result[:])

@@ -44,19 +44,17 @@ def tile_list_tabw_tm_gelu_kernel(tc, tab, w, b, offs, out):
         ident = keep.tile([P, P], F32, align_bytes=64, name="ident")
         warm = keep.tile([P, 1], F32, name="warm")
 
-        nc.vector.memset(planes[:, 0:2560].bitcast(I32), 0)
-        nc.gpsimd.memset(planes[:, 2560:T].bitcast(I32), 0)
-        nc.gpsimd.memset(b_rows[:], 0.0)
+        nc.vector.memset(planes[:].bitcast(I32), 0)
         nc.gpsimd.memset(warm[:], 0.0)
-        make_identity(nc, ident[:])
         nc.sync.dma_start(offsets[:], offs)
         scale_rows = tab[:, 512 * T : 528 * T].rearrange("a (q t) -> a q t", t=T)
         for quad in range(4):
-            queue = nc.sync if quad < 2 else nc.scalar
+            queue = nc.scalar if quad < 2 else nc.gpsimd
             queue.dma_start(
                 out=planes[32 * quad : 32 * quad + 4 * PASSES, :].bitcast(I32),
                 in_=scale_rows[:, 4 * quad : 4 * quad + 4, :].bitcast(I32),
             )
+        nc.scalar.activation(warm[:], warm[:], GELU)
 
         def load_words(a):
             nc.sync.dma_start(out=words[a][:], in_=tab[a, 0 : 512 * T].rearrange("(p x) -> p x", p=P).bitcast(I32))
@@ -64,13 +62,14 @@ def tile_list_tabw_tm_gelu_kernel(tc, tab, w, b, offs, out):
         def load_w(a):
             nc.sync.dma_start(out=w_raw[a][:], in_=w[512 * a : 512 * (a + 1), :].rearrange("(p j) n -> p j n", j=4))
 
-        nc.scalar.activation(warm[:], warm[:], GELU)
         load_words(0)
+        nc.gpsimd.memset(b_rows[:], 0.0)
+        make_identity(nc, ident[:])
         nc.scalar.dma_start(out=b_rows[0 : N // P, :], in_=b.rearrange("(c p) -> c p", p=P))
         load_words(1)
         load_w(0)
-        load_words(2)
         load_w(1)
+        load_words(2)
         load_w(2)
 
         turned = psum.tile([P, N], F32, name="acc")
@@ -113,24 +112,34 @@ def tile_list_tabw_tm_gelu_kernel(tc, tab, w, b, offs, out):
                 stop=(a == PASSES - 1),
             )
 
-        gather_planes(0, S)
-        gather_words(0, 0, S)
-        gather_words(1, 0, S)
-        group(nc.scalar.copy, 0, 0, N)
+        def finish(acc, i, parts):
+            for c in range(parts):
+                cols = slice(N // parts * c, N // parts * (c + 1))
+                summed = stage.tile([P, N // parts], F32, name="summed")
+                nc.vector.tensor_tensor(summed[:], acc[:, cols], bias[:, cols], ADD)
+                result = stage.tile([P, N // parts], F32, name="result")
+                nc.scalar.activation(result[:], summed[:], GELU)
+                nc.sync.dma_start(out=out[P * i : P * (i + 1), cols], in_=result[:])
+
+        group(nc.scalar.copy, 0, 0, 512)
         quantize(0)
+        group(nc.scalar.copy, 1, 0, 400)
+        group(pool_copy, 1, 400, 512)
+        quantize(1)
+        group(nc.scalar.copy, 2, 0, 352)
+        group(pool_copy, 2, 352, 432)
+        group(nc.vector.tensor_copy, 2, 432, 512)
+        quantize(2)
+        gather_planes(0, S)
+        for j0 in (0, S // 2):
+            for a in range(PASSES - 1):
+                gather_words(a, j0, j0 + S // 2)
         accs = [psum.tile([P, N], F32, name="acc") for i in range(BANKS)]
-        for i in range(BANKS):
-            multiply(accs[i], i, 0)
         for j0 in range(0, S, 512):
             gather_words(2, j0, j0 + 512)
-        group(nc.scalar.copy, 1, 0, 400)
-        group(pool_copy, 1, 400, N)
-        quantize(1)
-        for i in range(BANKS):
-            multiply(accs[i], i, 1)
-        group(nc.scalar.copy, 2, 0, 400)
-        group(pool_copy, 2, 400, N)
-        quantize(2)
+        for a in range(PASSES - 1):
+            for i in range(BANKS):
+                multiply(accs[i], i, a)
         for i in range(TILES):
             if i < BANKS:
                 acc = accs[i]
@@ -139,11 +148,4 @@ def tile_list_tabw_tm_gelu_kernel(tc, tab, w, b, offs, out):
                 multiply(acc, i, 0)
                 multiply(acc, i, 1)
             multiply(acc, i, 2)
-            parts = 1 if i < TILES - 1 else 2
-            for c in range(parts):
-                cols = slice(N // parts * c, N // parts * (c + 1))
-                summed = stage.tile([P, N // parts], F32, name="summed")
-                nc.vector.tensor_tensor(summed[:], acc[:, cols], bias[:, cols], ADD)
-                result = stage.tile([P, N // parts], F32, name="result")
-                nc.scalar.activation(result[:], summed[:], GELU)
-                nc.sync.dma_start(out=out[P * i : P * (i + 1), cols], in_=result[:])
+            finish(acc, i, 1 if i < TILES - 1 else 2)

@@ -17,8 +17,8 @@ GELU = mybir.ActivationFunctionType.Gelu_apprx_tanh
 K, N, T, S = 1536, 512, 4096, 2048
 P = 128
 PASSES = K // 512
-TILES = S // P
-BANKS = 8
+H = N // 2
+PAIRS = S // (2 * P)
 FLOPS = 2 * K * N * S
 
 
@@ -26,51 +26,44 @@ def tile_list_tabw_tm_gelu_kernel(tc, tab, w, b, offs, out):
     nc = tc.nc
     with ExitStack() as ctx:
         keep = ctx.enter_context(tc.tile_pool(name="keep", bufs=1))
+        turns = ctx.enter_context(tc.tile_pool(name="turns", bufs=1))
         stage = ctx.enter_context(tc.tile_pool(name="stage", bufs=8))
-        psum = ctx.enter_context(tc.psum_pool(name="psum", bufs=BANKS))
+        psum = ctx.enter_context(tc.psum_pool(name="psum", bufs=PAIRS))
 
         offsets = keep.tile([P, S // 16], U16, name="offsets")
         planes = keep.tile([P, T], U8, align_bytes=64, name="planes")
-        words = [keep.tile([P, T], I32, align_bytes=64, name=f"words{a}") for a in range(PASSES)]
-        w_raw = [keep.tile([P, 4, N], F32, align_bytes=64, name=f"w_raw{a}") for a in range(PASSES)]
+        words = [turns.tile([P, T], I32, align_bytes=64, name="words_even")]
+        words.append(keep.tile([P, T], I32, align_bytes=64, name="words_odd"))
         w_grp = [keep.tile([P, N, 4], BF16, align_bytes=64, name=f"w_grp{a}") for a in range(PASSES)]
         w_codes = [keep.tile([P, N], U32, align_bytes=64, name=f"w_codes{a}") for a in range(PASSES)]
         w_scales = [keep.tile([P, N], U8, align_bytes=64, name=f"w_scales{a}") for a in range(PASSES)]
         g_words = [keep.tile([P, S], U32, align_bytes=64, name=f"g_words{a}") for a in range(PASSES)]
         g_planes = keep.tile([P, S], U8, align_bytes=64, name="g_planes")
-        bias = keep.tile([P, N], F32, align_bytes=64, name="bias")
-        b_rows = keep.tile([P, P], F32, align_bytes=64, name="b_rows")
-        b_cols = keep.tile([P, N // P], F32, align_bytes=64, name="b_cols")
-        ident = keep.tile([P, P], F32, align_bytes=64, name="ident")
+        bias = keep.tile([P, 2, 2, H], F32, align_bytes=64, name="bias")
+        b_rows = turns.tile([P, P], F32, align_bytes=64, name="turn0")
+        b_cols = turns.tile([P, N // P], F32, align_bytes=64, name="turn1")
+        ident = turns.tile([P, P], F32, align_bytes=64, name="turn2")
         warm = keep.tile([P, 1], F32, name="warm")
 
+        nc.gpsimd.memset(b_rows[:], 0.0)
         nc.vector.memset(planes[:].bitcast(I32), 0)
         nc.gpsimd.memset(warm[:], 0.0)
         nc.sync.dma_start(offsets[:], offs)
-        scale_rows = tab[:, 512 * T : 528 * T].rearrange("a (q t) -> a q t", t=T)
-        for quad in range(4):
-            queue = nc.scalar if quad < 2 else nc.gpsimd
-            queue.dma_start(
-                out=planes[32 * quad : 32 * quad + 4 * PASSES, :].bitcast(I32),
-                in_=scale_rows[:, 4 * quad : 4 * quad + 4, :].bitcast(I32),
-            )
-        nc.scalar.activation(warm[:], warm[:], GELU)
+        nc.sync.dma_start(out=b_rows[0 : N // P, :], in_=b.rearrange("(c p) -> c p", p=P))
 
         def load_words(a):
             nc.sync.dma_start(out=words[a][:], in_=tab[a, 0 : 512 * T].rearrange("(p x) -> p x", p=P).bitcast(I32))
 
-        def load_w(a):
-            nc.sync.dma_start(out=w_raw[a][:], in_=w[512 * a : 512 * (a + 1), :].rearrange("(p j) n -> p j n", j=4))
-
         load_words(0)
-        nc.gpsimd.memset(b_rows[:], 0.0)
-        make_identity(nc, ident[:])
-        nc.scalar.dma_start(out=b_rows[0 : N // P, :], in_=b.rearrange("(c p) -> c p", p=P))
         load_words(1)
-        load_w(0)
-        load_w(1)
-        load_words(2)
-        load_w(2)
+        scale_rows = tab[:, 512 * T : 528 * T].rearrange("a (q t) -> a q t", t=T)
+        for quad in range(4):
+            nc.gpsimd.dma_start(
+                out=planes[32 * quad : 32 * quad + 4 * PASSES, :].bitcast(I32),
+                in_=scale_rows[:, 4 * quad : 4 * quad + 4, :].bitcast(I32),
+            )
+        make_identity(nc, ident[:])
+        nc.scalar.activation(warm[:], warm[:], GELU)
 
         turned = psum.tile([P, N], F32, name="acc")
         nc.tensor.transpose(turned[:, 0:P], b_rows[:], ident[:])
@@ -78,74 +71,87 @@ def tile_list_tabw_tm_gelu_kernel(tc, tab, w, b, offs, out):
         spread = psum.tile([P, N], F32, name="acc")
         for c in range(N // P):
             nc.tensor.transpose(spread[:, P * c : P * (c + 1)], b_cols[:, c : c + 1].to_broadcast([P, P]), ident[:])
-        nc.scalar.copy(bias[:], spread[:])
+        for u in range(2):
+            nc.scalar.copy(bias[:, :, u, :], spread[:].rearrange("p (h n) -> p h n", h=2))
 
-        def gather_planes(j0, j1):
-            nc.vector.tensor_copy(g_planes[:, j0:j1], planes[:].indirect(offsets[:, j0 // 16 : j1 // 16]))
+        def gather_planes():
+            nc.vector.tensor_copy(g_planes[:], planes[:].indirect(offsets[:]))
 
         def gather_words(a, j0, j1):
             nc.vector.tensor_copy(g_words[a][:, j0:j1], words[a][:].bitcast(U32).indirect(offsets[:, j0 // 16 : j1 // 16]))
 
-        def group(engine_copy, a, n0, n1):
-            engine_copy(
-                w_grp[a][:, n0:n1, :].rearrange("p (c i) t -> p c t i", i=4),
-                w_raw[a][:, :, n0:n1].rearrange("p t (c i) -> p c t i", i=4),
-            )
-
         def pool_copy(dst, src):
             nc.gpsimd.tensor_scalar(dst, src, 1.0, 0.0, MULT, ADD)
 
-        def quantize(a):
+        def prepare(a, h, by_scalar):
+            raw = turns.tile([P, 4, H], F32, align_bytes=64, name=f"turn{a}")
+            nc.sync.dma_start(
+                out=raw[:], in_=w[512 * a : 512 * (a + 1), H * h : H * (h + 1)].rearrange("(p j) n -> p j n", j=4)
+            )
+            for engine_copy, n0, n1 in ((nc.scalar.copy, 0, by_scalar), (pool_copy, by_scalar, H)):
+                engine_copy(
+                    w_grp[a][:, H * h + n0 : H * h + n1, :].rearrange("p (c i) t -> p c t i", i=4),
+                    raw[:, :, n0:n1].rearrange("p t (c i) -> p c t i", i=4),
+                )
+            cols = slice(H * h, H * (h + 1))
             nc.vector.quantize_mx(
-                out=w_codes[a][:].bitcast(FP8X4), scales=w_scales[a][:], in_=w_grp[a][:].rearrange("p n t -> p (n t)")
+                out=w_codes[a][:, cols].bitcast(FP8X4),
+                scales=w_scales[a][:, cols],
+                in_=w_grp[a][:, cols, :].rearrange("p n t -> p (n t)"),
             )
 
-        def multiply(acc, i, a):
-            cols = slice(P * i, P * (i + 1))
+        def multiply(acc, i, h, a):
+            tokens = slice(P * i, P * (i + 1))
+            cols = slice(H * h, H * (h + 1))
             nc.tensor.matmul_mx(
-                out=acc[:],
-                lhsT=g_words[a][:, cols].bitcast(FP8X4),
-                lhsT_scale=g_planes[4 * a : P, cols],
-                rhs=w_codes[a][:].bitcast(FP8X4),
-                rhs_scale=w_scales[a][:],
+                out=acc[:, H * (i % 2) : H * (i % 2 + 1)],
+                lhsT=g_words[a][:, tokens].bitcast(FP8X4),
+                lhsT_scale=g_planes[4 * a : P, tokens],
+                rhs=w_codes[a][:, cols].bitcast(FP8X4),
+                rhs_scale=w_scales[a][:, cols],
                 start=(a == 0),
                 stop=(a == PASSES - 1),
             )
 
-        def finish(acc, i, parts):
-            for c in range(parts):
-                cols = slice(N // parts * c, N // parts * (c + 1))
-                summed = stage.tile([P, N // parts], F32, name="summed")
-                nc.vector.tensor_tensor(summed[:], acc[:, cols], bias[:, cols], ADD)
-                result = stage.tile([P, N // parts], F32, name="result")
+        def finish(acc, pair, h, tiles):
+            for us in tiles:
+                part = slice(H * us[0], H * (us[-1] + 1))
+                width = H * len(us)
+                summed = stage.tile([P, width], F32, name="summed")
+                nc.vector.tensor_tensor(
+                    summed[:], acc[:, part], bias[:, h, us[0] : us[-1] + 1, :].rearrange("p u n -> p (u n)"), ADD
+                )
+                result = stage.tile([P, width], F32, name="result")
                 nc.scalar.activation(result[:], summed[:], GELU)
-                nc.sync.dma_start(out=out[P * i : P * (i + 1), cols], in_=result[:])
+                t0 = 2 * P * pair + P * us[0]
+                nc.sync.dma_start(
+                    out=out[t0 : t0 + P * len(us), H * h : H * (h + 1)].rearrange("(u q) n -> q u n", q=P),
+                    in_=result[:].rearrange("p (u n) -> p u n", n=H),
+                )
 
-        group(nc.scalar.copy, 0, 0, 512)
-        quantize(0)
-        group(nc.scalar.copy, 1, 0, 400)
-        group(pool_copy, 1, 400, 512)
-        quantize(1)
-        group(nc.scalar.copy, 2, 0, 352)
-        group(pool_copy, 2, 352, 432)
-        group(nc.vector.tensor_copy, 2, 432, 512)
-        quantize(2)
-        gather_planes(0, S)
-        for j0 in (0, S // 2):
-            for a in range(PASSES - 1):
-                gather_words(a, j0, j0 + S // 2)
-        accs = [psum.tile([P, N], F32, name="acc") for i in range(BANKS)]
-        for j0 in range(0, S, 512):
-            gather_words(2, j0, j0 + 512)
+        for a in range(PASSES):
+            prepare(a, 0, 208)
+        gather_words(0, 0, S)
+        gather_words(1, 0, S)
+        gather_planes()
+        words.append(turns.tile([P, T], I32, align_bytes=64, name="words_even"))
+        load_words(2)
+        for a in range(PASSES):
+            prepare(a, 1, 160)
+        accs = [psum.tile([P, N], F32, name="acc") for pair in range(PAIRS)]
         for a in range(PASSES - 1):
-            for i in range(BANKS):
-                multiply(accs[i], i, a)
-        for i in range(TILES):
-            if i < BANKS:
-                acc = accs[i]
-            else:
-                acc = psum.tile([P, N], F32, name="acc")
-                multiply(acc, i, 0)
-                multiply(acc, i, 1)
-            multiply(acc, i, 2)
-            finish(acc, i, 1 if i < TILES - 1 else 2)
+            for pair in range(PAIRS):
+                multiply(accs[pair], 2 * pair, 0, a)
+        for pair in range(PAIRS):
+            if pair % 2 == 0:
+                gather_words(2, 2 * P * pair, 2 * P * (pair + 2))
+            multiply(accs[pair], 2 * pair, 0, PASSES - 1)
+            for a in range(PASSES):
+                multiply(accs[pair], 2 * pair + 1, 0, a)
+            finish(accs[pair], pair, 0, ((0, 1),))
+        for pair in range(PAIRS):
+            acc = psum.tile([P, N], F32, name="acc")
+            for u in range(2):
+                for a in range(PASSES):
+                    multiply(acc, 2 * pair + u, 1, a)
+            finish(acc, pair, 1, ((0, 1),) if pair < PAIRS - 1 else ((0,), (1,)))

from contextlib import ExitStack

import concourse.mybir as mybir
from concourse.masks import make_identity

F32 = mybir.dt.float32
BF16 = mybir.dt.bfloat16
I32 = mybir.dt.int32
U32 = mybir.dt.uint32
U16 = mybir.dt.uint16
U8 = mybir.dt.uint8
FP8X4 = mybir.dt.float8_e4m3fn_x4
ADD = mybir.AluOpType.add
MULT = mybir.AluOpType.mult
GELU = mybir.ActivationFunctionType.Gelu_apprx_tanh

K, N, T, S = 1536, 512, 4096, 2048
P = 128
PASSES = K // 512
H = N // 2
PAIRS = S // (2 * P)
FLOPS = 2 * K * N * S


def tile_list_tabw_tm_gelu_kernel(tc, tab, w, b, offs, out):
    nc = tc.nc
    with ExitStack() as ctx:
        keep = ctx.enter_context(tc.tile_pool(name="keep", bufs=1))
        turns = ctx.enter_context(tc.tile_pool(name="turns", bufs=1))
        stage = ctx.enter_context(tc.tile_pool(name="stage", bufs=8))
        psum = ctx.enter_context(tc.psum_pool(name="psum", bufs=PAIRS))

        offsets = keep.tile([P, S // 16], U16, name="offsets")
        planes = keep.tile([P, T], U8, align_bytes=64, name="planes")
        words = [turns.tile([P, T], I32, align_bytes=64, name="words_even")]
        words.append(keep.tile([P, T], I32, align_bytes=64, name="words_odd"))
        w_grp = [keep.tile([P, N, 4], BF16, align_bytes=64, name=f"w_grp{a}") for a in range(PASSES)]
        w_codes = [keep.tile([P, N], U32, align_bytes=64, name=f"w_codes{a}") for a in range(PASSES)]
        w_scales = [keep.tile([P, N], U8, align_bytes=64, name=f"w_scales{a}") for a in range(PASSES)]
        g_words = [keep.tile([P, S], U32, align_bytes=64, name=f"g_words{a}") for a in range(PASSES)]
        g_planes = keep.tile([P, S], U8, align_bytes=64, name="g_planes")
        bias = keep.tile([P, 2, 2, H], F32, align_bytes=64, name="bias")
        b_rows = turns.tile([P, P], F32, align_bytes=64, name="turn0")
        b_cols = turns.tile([P, N // P], F32, align_bytes=64, name="turn1")
        ident = turns.tile([P, P], F32, align_bytes=64, name="turn2")
        warm = keep.tile([P, 1], F32, name="warm")

        nc.gpsimd.memset(b_rows[:], 0.0)
        nc.vector.memset(planes[:].bitcast(I32), 0)
        nc.gpsimd.memset(warm[:], 0.0)
        nc.sync.dma_start(offsets[:], offs)
        nc.sync.dma_start(out=b_rows[0 : N // P, :], in_=b.rearrange("(c p) -> c p", p=P))

        def load_words(a):
            nc.sync.dma_start(out=words[a][:], in_=tab[a, 0 : 512 * T].rearrange("(p x) -> p x", p=P).bitcast(I32))

        load_words(0)
        load_words(1)
        scale_rows = tab[:, 512 * T : 528 * T].rearrange("a (q t) -> a q t", t=T)
        for quad in range(4):
            nc.gpsimd.dma_start(
                out=planes[32 * quad : 32 * quad + 4 * PASSES, :].bitcast(I32),
                in_=scale_rows[:, 4 * quad : 4 * quad + 4, :].bitcast(I32),
            )
        make_identity(nc, ident[:])
        nc.scalar.activation(warm[:], warm[:], GELU)

        turned = psum.tile([P, N], F32, name="acc")
        nc.tensor.transpose(turned[:, 0:P], b_rows[:], ident[:])
        nc.scalar.copy(b_cols[:], turned[:, 0 : N // P])
        spread = psum.tile([P, N], F32, name="acc")
        for c in range(N // P):
            nc.tensor.transpose(spread[:, P * c : P * (c + 1)], b_cols[:, c : c + 1].to_broadcast([P, P]), ident[:])
        for u in range(2):
            nc.scalar.copy(bias[:, :, u, :], spread[:].rearrange("p (h n) -> p h n", h=2))

        def gather_planes():
            nc.vector.tensor_copy(g_planes[:], planes[:].indirect(offsets[:]))

        def gather_words(a, j0, j1):
            nc.vector.tensor_copy(g_words[a][:, j0:j1], words[a][:].bitcast(U32).indirect(offsets[:, j0 // 16 : j1 // 16]))

        def pool_copy(dst, src):
            nc.gpsimd.tensor_scalar(dst, src, 1.0, 0.0, MULT, ADD)

        def prepare(a, h, by_scalar):
            raw = turns.tile([P, 4, H], F32, align_bytes=64, name=f"turn{a}")
            nc.sync.dma_start(
                out=raw[:], in_=w[512 * a : 512 * (a + 1), H * h : H * (h + 1)].rearrange("(p j) n -> p j n", j=4)
            )
            for engine_copy, n0, n1 in ((nc.scalar.copy, 0, by_scalar), (pool_copy, by_scalar, H)):
                engine_copy(
                    w_grp[a][:, H * h + n0 : H * h + n1, :].rearrange("p (c i) t -> p c t i", i=4),
                    raw[:, :, n0:n1].rearrange("p t (c i) -> p c t i", i=4),
                )
            cols = slice(H * h, H * (h + 1))
            nc.vector.quantize_mx(
                out=w_codes[a][:, cols].bitcast(FP8X4),
                scales=w_scales[a][:, cols],
                in_=w_grp[a][:, cols, :].rearrange("p n t -> p (n t)"),
            )

        def multiply(acc, i, h, a):
            tokens = slice(P * i, P * (i + 1))
            cols = slice(H * h, H * (h + 1))
            nc.tensor.matmul_mx(
                out=acc[:, H * (i % 2) : H * (i % 2 + 1)],
                lhsT=g_words[a][:, tokens].bitcast(FP8X4),
                lhsT_scale=g_planes[4 * a : P, tokens],
                rhs=w_codes[a][:, cols].bitcast(FP8X4),
                rhs_scale=w_scales[a][:, cols],
                start=(a == 0),
                stop=(a == PASSES - 1),
            )

        def finish(acc, pair, h, tiles):
            for us in tiles:
                part = slice(H * us[0], H * (us[-1] + 1))
                width = H * len(us)
                summed = stage.tile([P, width], F32, name="summed")
                nc.vector.tensor_tensor(
                    summed[:], acc[:, part], bias[:, h, us[0] : us[-1] + 1, :].rearrange("p u n -> p (u n)"), ADD
                )
                result = stage.tile([P, width], F32, name="result")
                nc.scalar.activation(result[:], summed[:], GELU)
                t0 = 2 * P * pair + P * us[0]
                nc.sync.dma_start(
                    out=out[t0 : t0 + P * len(us), H * h : H * (h + 1)].rearrange("(u q) n -> q u n", q=P),
                    in_=result[:].rearrange("p (u n) -> p u n", n=H),
                )

        for a in range(PASSES):
            prepare(a, 0, 208)
        gather_words(0, 0, S)
        gather_words(1, 0, S)
        gather_planes()
        words.append(turns.tile([P, T], I32, align_bytes=64, name="words_even"))
        load_words(2)
        for a in range(PASSES):
            prepare(a, 1, 160)
        accs = [psum.tile([P, N], F32, name="acc") for pair in range(PAIRS)]
        for a in range(PASSES - 1):
            for pair in range(PAIRS):
                multiply(accs[pair], 2 * pair, 0, a)
        for pair in range(PAIRS):
            if pair % 2 == 0:
                gather_words(2, 2 * P * pair, 2 * P * (pair + 2))
            multiply(accs[pair], 2 * pair, 0, PASSES - 1)
            for a in range(PASSES):
                multiply(accs[pair], 2 * pair + 1, 0, a)
            finish(accs[pair], pair, 0, ((0, 1),))
        for pair in range(PAIRS):
            acc = psum.tile([P, N], F32, name="acc")
            for u in range(2):
                for a in range(PASSES):
                    multiply(acc, 2 * pair + u, 1, a)
            finish(acc, pair, 1, ((0, 1),) if pair < PAIRS - 1 else ((0,), (1,)))
